import numpy as np
import ml_dtypes


def mxq(x, axis, fmt="e4m3"):
    dtype, down = {"e4m3": (ml_dtypes.float8_e4m3fn, 7), "e5m2": (ml_dtypes.float8_e5m2, 14)}[fmt]
    v = np.moveaxis(np.asarray(x, np.float32).astype(ml_dtypes.bfloat16).astype(np.float64), axis, -1)
    blocks = v.reshape(v.shape[:-1] + (-1, 32))
    amax = np.abs(blocks).max(-1, keepdims=True)
    byte = np.maximum(np.where(amax > 0, np.frexp(amax)[1] - 1 + 127, 0) - down, 1)
    scale = np.exp2(byte - 127.0)
    codes = (blocks / scale).astype(np.float32).astype(dtype).astype(np.float64)
    return np.moveaxis((codes * scale).reshape(v.shape), -1, axis)


WIDE = False


def mx_kscale(k):
    if not WIDE:
        return np.ones(k)
    levels = np.array([30, -30])
    if k % 512:
        return np.exp2(np.random.permutation(np.resize(levels, k // 32))).repeat(32)
    a = np.empty((k // 512, 16))
    for p in range(k // 512):
        a[p, :8] = np.random.permutation(np.resize(levels, 8))
        for g in range(8):
            far = levels[np.abs(levels - a[p, g]) >= 10]
            a[p, g + 8] = far[np.random.randint(len(far))]
    return np.exp2(a.ravel()).repeat(32)


def f64(x):
    return np.asarray(x).astype(np.float64)


def striped(idx):
    return np.tile(np.asarray(idx).reshape(-1, 16).T, (8, 1)).astype(np.uint16)


def unstriped(offs):
    return offs[:16].T.reshape(-1).astype(np.int64)


E2M1 = np.array([0.0, 0.5, 1.0, 1.5, 2.0, 3.0, 4.0, 6.0, -0.0, -0.5, -1.0, -1.5, -2.0, -3.0, -4.0, -6.0])


def pack_weight(w, fmt):
    k, n = w.shape
    w = f64(np.asarray(w, np.float32).astype(ml_dtypes.bfloat16)).reshape(k // 32, 32, n)
    amax = np.abs(w).max(1)
    if fmt in ("e4m3", "e5m2"):
        byte = np.frexp(amax)[1] - 1 + 127 - (7 if fmt == "e4m3" else 14)
    else:
        mant, ex = np.frexp(amax / 6.0)
        byte = np.where(mant > 0.5, ex, ex - 1) + 127
    byte = np.clip(np.where(amax > 0, byte, 1), 1, 254)
    scaled = (w * np.exp2(127.0 - byte)[:, None, :]).reshape(k, n).astype(np.float32)
    by_word = np.ascontiguousarray(scaled.reshape(k // 512, 128, 4, n).transpose(0, 1, 3, 2))
    if fmt in ("e4m3", "e5m2"):
        words = by_word.astype(ml_dtypes.float8_e4m3fn if fmt == "e4m3" else ml_dtypes.float8_e5m2).view(np.uint8)
    else:
        c = by_word.astype(ml_dtypes.float4_e2m1fn).view(np.uint8) & 0xF
        words = (c[..., 0::2] | (c[..., 1::2] << 4)).reshape(k // 512, 128, 2 * n)
    return np.ascontiguousarray(words), np.ascontiguousarray(byte.astype(np.uint8).reshape(k // 512, 16, n))


def unpack_weight(words, scales, fmt):
    g, _, n = scales.shape
    words = np.ascontiguousarray(words).reshape(g, 128, n, -1)
    if fmt in ("e4m3", "e5m2"):
        vals = words.view(ml_dtypes.float8_e4m3fn if fmt == "e4m3" else ml_dtypes.float8_e5m2).astype(np.float64)
    else:
        nib = np.empty((g, 128, n, 4), np.uint8)
        nib[..., 0::2] = words & 0xF
        nib[..., 1::2] = words >> 4
        vals = E2M1[nib]
    vals = vals * np.repeat(np.exp2(scales.astype(np.float64) - 127.0), 8, axis=1)[..., None]
    return vals.transpose(0, 1, 3, 2).reshape(g * 512, n)


def sigmoid(v):
    return 1.0 / (1.0 + np.exp(-v))


def sgn(shape):
    return np.random.uniform(0.5, 2.0, shape) * np.where(np.random.standard_normal(shape) < 0, -1.0, 1.0)


K, T, J, R, F, Z, O, N = 512, 1024, 256, 512, 512, 1024, 128, 256


def setup_inputs():
    n = np.random.standard_normal
    idx = np.random.permutation(T)[:J]
    idx2 = np.random.permutation(Z)[:J]
    idx3 = np.random.permutation(J)[:O]
    idx4 = np.random.permutation(J)[:O]
    idx5 = np.random.permutation(J)[:O]
    idx6 = np.random.permutation(J)[:O]
    idx7 = np.random.permutation(T)[:O]
    fk = mx_kscale(K)
    ff = mx_kscale(F)
    fr = mx_kscale(R)
    xtp = pack_weight(n((K, T)) / fk[:, None], "e4m3")
    xop = pack_weight(n((F, Z)) / ff[:, None], "e2m1")
    wp = pack_weight(n((K, R)) * 1 / np.sqrt(K) * fk[:, None], "e2m1")
    w2p = pack_weight(n((F, R)) * 1 / np.sqrt(F) * ff[:, None], "e5m2")
    wbp = pack_weight(n((R, N)) * 1 / np.sqrt(R) / fr[:, None], "e5m2")
    wsp = pack_weight(n((K, N)) * 1 / np.sqrt(K) * fk[:, None], "e5m2")
    return {
        "xt_words": xtp[0],
        "xt_scales": xtp[1],
        "xo_words": xop[0],
        "xo_scales": xop[1],
        "w_words": wp[0],
        "w_scales": wp[1],
        "w2_words": w2p[0],
        "w2_scales": w2p[1],
        "sa": (np.random.uniform(0.5, 1.6, (R, 1)) * fr[:, None]).astype(np.float32),
        "sb": (np.random.uniform(0.5, 1.6, (R, 1)) * fr[:, None]).astype(np.float32),
        "sg": (sgn((R, 1))).astype(np.float32),
        "bg": (np.random.uniform(-2.0, 2.0, (R, 1))).astype(np.float32),
        "sh": (sgn((R, 1))).astype(np.float32),
        "bh": (np.random.uniform(-2.0, 2.0, (R, 1))).astype(np.float32),
        "wb_words": wbp[0],
        "wb_scales": wbp[1],
        "ws_words": wsp[0],
        "ws_scales": wsp[1],
        "offs": striped(idx),
        "offs2": striped(idx2),
        "offs3": striped(idx3),
        "offs4": striped(idx4),
        "offs5": striped(idx5),
        "offs6": striped(idx6),
        "offs7": striped(idx7),
    }


def reference(xt_words, xt_scales, xo_words, xo_scales, w_words, w_scales, w2_words, w2_scales, sa, sb, sg, bg, sh, bh, wb_words, wb_scales, ws_words, ws_scales, offs, offs2, offs3, offs4, offs5, offs6, offs7):
    idx = unstriped(offs)
    idx2 = unstriped(offs2)
    idx3 = unstriped(offs3)
    idx4 = unstriped(offs4)
    idx5 = unstriped(offs5)
    idx6 = unstriped(offs6)
    idx7 = unstriped(offs7)
    xtu = unpack_weight(xt_words, xt_scales, "e4m3")
    xou = unpack_weight(xo_words, xo_scales, "e2m1")
    wu = unpack_weight(w_words, w_scales, "e2m1")
    w2u = unpack_weight(w2_words, w2_scales, "e5m2")
    wbu = unpack_weight(wb_words, wb_scales, "e5m2")
    wsu = unpack_weight(ws_words, ws_scales, "e5m2")
    xtidxg = xtu[:, idx]
    a = wu.T @ xtidxg
    xoidx2g = xou[:, idx2]
    b = w2u.T @ xoidx2g
    u1 = a[:, idx3] * f64(sa) * sigmoid(b[:, idx4] * f64(sg) + f64(bg))
    u2 = b[:, idx5] * f64(sb) * sigmoid(a[:, idx6] * f64(sh) + f64(bh))
    hid = np.abs(u1 - u2)
    hidq = mxq(hid, 0, "e4m3")
    xtidx7g = xtu[:, idx7]
    y = wbu.T @ hidq + wsu.T @ xtidx7g
    return y

@@ -1,0 +1,169 @@
+from contextlib import ExitStack
+
+import concourse.mybir as mybir
+
+F32 = mybir.dt.float32
+BF16 = mybir.dt.bfloat16
+I32 = mybir.dt.int32
+U32 = mybir.dt.uint32
+U16 = mybir.dt.uint16
+U8 = mybir.dt.uint8
+E4M3 = mybir.dt.float8_e4m3fn_x4
+E5M2 = mybir.dt.float8_e5m2_x4
+E2M1 = mybir.dt.float4_e2m1fn_x4
+ACT = mybir.ActivationFunctionType
+ALU = mybir.AluOpType
+
+P = 128
+PACK = 4
+T, J, R, Z, O, N = 1024, 256, 512, 1024, 128, 256
+FLOPS = 335544320
+
+
+def tile_list_gatedcross_twotab_further_plain_kernel(
+    tc, xt_words, xt_scales, xo_words, xo_scales, w_words, w_scales, w2_words, w2_scales,
+    sa, sb, sg, bg, sh, bh, wb_words, wb_scales, ws_words, ws_scales,
+    offs, offs2, offs3, offs4, offs5, offs6, offs7, out,
+):
+    nc = tc.nc
+    with ExitStack() as ctx:
+        keep = ctx.enter_context(tc.tile_pool(name="keep", bufs=1))
+        psum = ctx.enter_context(tc.psum_pool(name="psum", bufs=1))
+
+        def tile(name, shape, dtype):
+            return keep.tile(shape, dtype, name=name, align_bytes=64)
+
+        def load_list(name, src):
+            dst = keep.tile(list(src.shape), U16, name=name)
+            nc.sync.dma_start(dst[:], src)
+            return dst
+
+        def load_words(queue, name, src, columns, dtype):
+            dst = tile(name, [P, columns], dtype)
+            queue.dma_start(dst[:].bitcast(I32), src.bitcast(I32))
+            return dst
+
+        def zeroed_plane(name, columns):
+            plane = tile(name, [P, columns], U8)
+            nc.vector.memset(plane[:].bitcast(I32), 0)
+            return plane
+
+        def load_plane(plane, src):
+            for q in range(4):
+                nc.sync.dma_start(plane[32 * q : 32 * q + 4, :].bitcast(I32), src[0, 4 * q : 4 * q + 4, :].bitcast(I32))
+
+        def load_rows(name, src):
+            dst = keep.tile([P, PACK], F32, name=name)
+            nc.gpsimd.dma_start(dst[:], src.rearrange("(p t) one -> p (t one)", t=PACK))
+            return dst
+
+        def deal(copy, name, src, dtype):
+            dst = tile(name, [P, R], dtype)
+            copy(dst[:].rearrange("p (t m) -> p m t", t=PACK), src[:].rearrange("p (m t) -> p m t", t=PACK))
+            return dst
+
+        def gather(name, window, offsets, count, dtype):
+            dst = tile(name, [P, count], dtype)
+            nc.vector.tensor_copy(dst[:], window[:].indirect(offsets[:]))
+            return dst
+
+        def flat(words):
+            return words[0].rearrange("p n t -> p (n t)")
+
+        xo_s = zeroed_plane("xo_s", Z)
+        w2_s = zeroed_plane("w2_s", R)
+        xt_s = zeroed_plane("xt_s", T)
+        w_s = zeroed_plane("w_s", R)
+        ws_s = zeroed_plane("ws_s", N)
+        wb_s = zeroed_plane("wb_s", N)
+
+        l2 = load_list("l2", offs2)
+        xo_w = load_words(nc.scalar, "xo_w", xo_words[0], Z, U16)
+        w2_stage = tile("w2_stage", [4, 4, R], U8)
+        nc.sync.dma_start(w2_stage[:].bitcast(I32), w2_scales[0].rearrange("(q r) n -> r q n", r=4).bitcast(I32))
+        w2_w = load_words(nc.scalar, "w2_w", flat(w2_words), R, U32)
+        load_plane(xo_s, xo_scales)
+        sg_t, bg_t, sb_t = load_rows("sg_t", sg), load_rows("bg_t", bg), load_rows("sb_t", sb)
+        xt_w = load_words(nc.scalar, "xt_w", flat(xt_words), T, U32)
+        w_w = load_words(nc.scalar, "w_w", w_words[0], R, U16)
+        l1 = load_list("l1", offs)
+        load_plane(xt_s, xt_scales)
+        l4 = load_list("l4", offs4)
+        l5 = load_list("l5", offs5)
+        load_plane(w_s, w_scales)
+        sh_t, bh_t, sa_t = load_rows("sh_t", sh), load_rows("bh_t", bh), load_rows("sa_t", sa)
+        l6 = load_list("l6", offs6)
+        l3 = load_list("l3", offs3)
+        l7 = load_list("l7", offs7)
+        ws_w = load_words(nc.sync, "ws_w", flat(ws_words), N, U32)
+        load_plane(ws_s, ws_scales)
+        wb_w = load_words(nc.sync, "wb_w", flat(wb_words), N, U32)
+        load_plane(wb_s, wb_scales)
+
+        for q in range(4):
+            nc.vector.tensor_copy(w2_s[32 * q : 32 * q + 4, :].bitcast(I32), w2_stage[:, q, :].bitcast(I32))
+        xo_gw = gather("xo_gw", xo_w, l2, J, U16)
+        w2_sd = deal(nc.vector.tensor_copy, "w2_sd", w2_s, U8)
+        xo_gs = gather("xo_gs", xo_s, l2, J, U8)
+        w2_wd = deal(nc.scalar.copy, "w2_wd", w2_w, U32)
+        w_wd = deal(nc.scalar.copy, "w_wd", w_w, U16)
+
+        def product(t, bank, name, wd, sd, wfmt, gw, gs, gfmt):
+            acc = psum.tile([P, J], F32, name=name + "_ps", tag="bank%d" % bank)
+            cols = slice(t * P, (t + 1) * P)
+            nc.tensor.matmul_mx(out=acc[:], lhsT=wd[:, cols].bitcast(wfmt), lhsT_scale=sd[:, cols],
+                                rhs=gw[:].bitcast(gfmt), rhs_scale=gs[:], start=True, stop=True)
+            rows = tile(name, [P, J], F32)
+            nc.vector.tensor_copy(rows[:], acc[:])
+            return rows
+
+        xt_gs = gather("xt_gs", xt_s, l1, J, U8)
+        b_rows = [product(t, t, "b%d" % t, w2_wd, w2_sd, E5M2, xo_gw, xo_gs, E2M1) for t in range(PACK)]
+        xt_gw = gather("xt_gw", xt_w, l1, J, U32)
+        w_sd = deal(nc.vector.tensor_copy, "w_sd", w_s, U8)
+        a_rows = [product(t, 4 + t, "a%d" % t, w_wd, w_sd, E2M1, xt_gw, xt_gs, E4M3) for t in range(PACK)]
+
+        x7_gw = gather("x7_gw", xt_w, l7, O, U32)
+        x7_gs = gather("x7_gs", xt_s, l7, O, U8)
+        y_ps = [psum.tile([P, O], F32, name="y%d_ps" % h, tag="bank%d" % h) for h in range(2)]
+        for h in range(2):
+            cols = slice(h * P, (h + 1) * P)
+            nc.tensor.matmul_mx(out=y_ps[h][:], lhsT=ws_w[:, cols].bitcast(E5M2), lhsT_scale=ws_s[:, cols],
+                                rhs=x7_gw[:].bitcast(E4M3), rhs_scale=x7_gs[:], start=True, stop=False)
+
+        val = [tile("val%d" % t, [P, 2, O], F32) for t in range(PACK)]
+        gate = [tile("gate%d" % t, [P, 2, O], F32) for t in range(PACK)]
+        for t in range(PACK):
+            nc.scalar.activation(gate[t][:, 0, :], b_rows[t][:].indirect(l4[:]), ACT.Sigmoid,
+                                 bias=bg_t[:, t : t + 1], scale=sg_t[:, t : t + 1])
+        for t in range(PACK):
+            nc.scalar.activation(val[t][:, 1, :], b_rows[t][:].indirect(l5[:]), ACT.Copy, scale=sb_t[:, t : t + 1])
+        diff = tile("diff", [P, PACK, O], F32)
+        for t in range(PACK):
+            nc.scalar.activation(gate[t][:, 1, :], a_rows[t][:].indirect(l6[:]), ACT.Sigmoid,
+                                 bias=bh_t[:, t : t + 1], scale=sh_t[:, t : t + 1])
+            nc.scalar.activation(val[t][:, 0, :], a_rows[t][:].indirect(l3[:]), ACT.Copy, scale=sa_t[:, t : t + 1])
+            u = tile("u%d" % t, [P, 2, O], F32)
+            if t < PACK - 1:
+                nc.vector.tensor_tensor(u[:], val[t][:], gate[t][:], ALU.mult)
+            else:
+                nc.vector.tensor_tensor(u[:, 1, :], val[t][:, 1, :], gate[t][:, 1, :], ALU.mult)
+                nc.vector.tensor_tensor(u[:, 0, :], val[t][:, 0, :], gate[t][:, 0, :], ALU.mult)
+            nc.vector.tensor_tensor(diff[:, t, :], u[:, 0, :], u[:, 1, :], ALU.subtract)
+
+        hid = tile("hid", [P, O, PACK], BF16)
+        for e in range(0, PACK, 2):
+            nc.scalar.activation(hid[:, :, e : e + 2], diff[:, e : e + 2, :].rearrange("p t o -> p o t"), ACT.Abs)
+        hid_w = tile("hid_w", [P, O], U32)
+        hid_s = tile("hid_s", [P, O], U8)
+        nc.vector.quantize_mx(out=hid_w[:].bitcast(E4M3), scales=hid_s[:], in_=hid[:].rearrange("p o t -> p (o t)"))
+
+        copies = (nc.vector.tensor_copy, nc.scalar.copy)
+        queues = (nc.sync, nc.scalar)
+        for h in range(2):
+            cols = slice(h * P, (h + 1) * P)
+            nc.tensor.matmul_mx(out=y_ps[h][:], lhsT=wb_w[:, cols].bitcast(E5M2), lhsT_scale=wb_s[:, cols],
+                                rhs=hid_w[:].bitcast(E4M3), rhs_scale=hid_s[:], start=False, stop=True)
+            y = tile("y%d" % h, [P, O], F32)
+            copies[h](y[:], y_ps[h][:])
+            queues[h].dma_start(out[cols, :], y[:])

@@ -38,9 +38,9 @@ def tile_list_gatedcross_twotab_further_plain_kernel(
             nc.sync.dma_start(dst[:], src)
             return dst
 
-        def load_words(queue, name, src, columns, dtype):
+        def load_words(name, src, columns, dtype):
             dst = tile(name, [P, columns], dtype)
-            queue.dma_start(dst[:].bitcast(I32), src.bitcast(I32))
+            nc.sync.dma_start(dst[:].bitcast(I32), src.bitcast(I32))
             return dst
 
         def zeroed_plane(name, columns):
@@ -48,19 +48,27 @@ def tile_list_gatedcross_twotab_further_plain_kernel(
             nc.vector.memset(plane[:].bitcast(I32), 0)
             return plane
 
+        def load_stage(name, src, columns):
+            stage = tile(name, [4, 4, columns], U8)
+            nc.sync.dma_start(stage[:].bitcast(I32), src[0].rearrange("(q r) n -> r q n", r=4).bitcast(I32))
+            return stage
+
+        def spread(plane, stage):
+            for q in range(4):
+                nc.vector.tensor_copy(plane[32 * q : 32 * q + 4, :].bitcast(I32), stage[:, q, :].bitcast(I32))
+
         def load_plane(plane, src):
             for q in range(4):
                 nc.sync.dma_start(plane[32 * q : 32 * q + 4, :].bitcast(I32), src[0, 4 * q : 4 * q + 4, :].bitcast(I32))
 
         def load_rows(name, src):
             dst = keep.tile([P, PACK], F32, name=name)
-            nc.gpsimd.dma_start(dst[:], src.rearrange("(p t) one -> p (t one)", t=PACK))
+            nc.sync.dma_start(dst[:], src.rearrange("(p t) one -> p (t one)", t=PACK))
             return dst
 
-        def deal(copy, name, src, dtype):
-            dst = tile(name, [P, R], dtype)
-            copy(dst[:].rearrange("p (t m) -> p m t", t=PACK), src[:].rearrange("p (m t) -> p m t", t=PACK))
-            return dst
+        def deal(copy, dst, src, slots):
+            by_slot = dst[:].rearrange("p (t m) -> p m t", t=PACK)
+            copy(by_slot[:, :, slots], src[:].rearrange("p (m t) -> p m t", t=PACK)[:, :, slots])
 
         def gather(name, window, offsets, count, dtype):
             dst = tile(name, [P, count], dtype)
@@ -77,36 +85,45 @@ def tile_list_gatedcross_twotab_further_plain_kernel(
         ws_s = zeroed_plane("ws_s", N)
         wb_s = zeroed_plane("wb_s", N)
 
+        warm = tile("warm", [P, 2], F32)
+        nc.vector.memset(warm[:, 0:1], 0.0)
+        nc.scalar.activation(warm[:, 1:2], warm[:, 0:1], ACT.Sigmoid)
+        w2_stage = load_stage("w2_stage", w2_scales, R)
+        xo_w = load_words("xo_w", xo_words[0], Z, U16)
         l2 = load_list("l2", offs2)
-        xo_w = load_words(nc.scalar, "xo_w", xo_words[0], Z, U16)
-        w2_stage = tile("w2_stage", [4, 4, R], U8)
-        nc.sync.dma_start(w2_stage[:].bitcast(I32), w2_scales[0].rearrange("(q r) n -> r q n", r=4).bitcast(I32))
-        w2_w = load_words(nc.scalar, "w2_w", flat(w2_words), R, U32)
         load_plane(xo_s, xo_scales)
-        sg_t, bg_t, sb_t = load_rows("sg_t", sg), load_rows("bg_t", bg), load_rows("sb_t", sb)
-        xt_w = load_words(nc.scalar, "xt_w", flat(xt_words), T, U32)
-        w_w = load_words(nc.scalar, "w_w", w_words[0], R, U16)
+        w2_w = load_words("w2_w", flat(w2_words), R, U32)
+        w_w = load_words("w_w", w_words[0], R, U16)
+        w_stage = load_stage("w_stage", w_scales, R)
+        l4 = load_list("l4", offs4)
+        sg_t, bg_t = load_rows("sg_t", sg), load_rows("bg_t", bg)
+        xt_w = load_words("xt_w", flat(xt_words), T, U32)
         l1 = load_list("l1", offs)
         load_plane(xt_s, xt_scales)
-        l4 = load_list("l4", offs4)
-        l5 = load_list("l5", offs5)
-        load_plane(w_s, w_scales)
-        sh_t, bh_t, sa_t = load_rows("sh_t", sh), load_rows("bh_t", bh), load_rows("sa_t", sa)
-        l6 = load_list("l6", offs6)
-        l3 = load_list("l3", offs3)
         l7 = load_list("l7", offs7)
-        ws_w = load_words(nc.sync, "ws_w", flat(ws_words), N, U32)
+        l5 = load_list("l5", offs5)
+        sb_t = load_rows("sb_t", sb)
+        l3 = load_list("l3", offs3)
+        sa_t = load_rows("sa_t", sa)
+        l6 = load_list("l6", offs6)
+        sh_t, bh_t = load_rows("sh_t", sh), load_rows("bh_t", bh)
+        ws_w = load_words("ws_w", flat(ws_words), N, U32)
+        wb_w = load_words("wb_w", flat(wb_words), N, U32)
         load_plane(ws_s, ws_scales)
-        wb_w = load_words(nc.sync, "wb_w", flat(wb_words), N, U32)
         load_plane(wb_s, wb_scales)
 
-        for q in range(4):
-            nc.vector.tensor_copy(w2_s[32 * q : 32 * q + 4, :].bitcast(I32), w2_stage[:, q, :].bitcast(I32))
+        spread(w2_s, w2_stage)
         xo_gw = gather("xo_gw", xo_w, l2, J, U16)
-        w2_sd = deal(nc.vector.tensor_copy, "w2_sd", w2_s, U8)
+        w2_sd, w2_wd = tile("w2_sd", [P, R], U8), tile("w2_wd", [P, R], U32)
+        w_sd, w_wd = tile("w_sd", [P, R], U8), tile("w_wd", [P, R], U16)
+        deal(nc.vector.tensor_copy, w2_sd, w2_s, slice(0, 2))
         xo_gs = gather("xo_gs", xo_s, l2, J, U8)
-        w2_wd = deal(nc.scalar.copy, "w2_wd", w2_w, U32)
-        w_wd = deal(nc.scalar.copy, "w_wd", w_w, U16)
+        deal(nc.vector.tensor_copy, w2_sd, w2_s, slice(2, 4))
+        deal(nc.scalar.copy, w2_wd, w2_w, slice(0, 2))
+        deal(nc.scalar.copy, w2_wd, w2_w, slice(2, 4))
+        deal(nc.scalar.copy, w_wd, w_w, slice(0, 4))
+        spread(w_s, w_stage)
+        nc.gpsimd.tensor_copy(w_sd[:].rearrange("p (t m) -> p t m", t=PACK), w_s[:].rearrange("p (m t) -> p t m", t=PACK))
 
         def product(t, bank, name, wd, sd, wfmt, gw, gs, gfmt):
             acc = psum.tile([P, J], F32, name=name + "_ps", tag="bank%d" % bank)
@@ -114,42 +131,40 @@ def tile_list_gatedcross_twotab_further_plain_kernel(
             nc.tensor.matmul_mx(out=acc[:], lhsT=wd[:, cols].bitcast(wfmt), lhsT_scale=sd[:, cols],
                                 rhs=gw[:].bitcast(gfmt), rhs_scale=gs[:], start=True, stop=True)
             rows = tile(name, [P, J], F32)
-            nc.vector.tensor_copy(rows[:], acc[:])
+            (nc.scalar.copy if name == "b0" else nc.vector.tensor_copy)(rows[:], acc[:])
             return rows
 
-        xt_gs = gather("xt_gs", xt_s, l1, J, U8)
         b_rows = [product(t, t, "b%d" % t, w2_wd, w2_sd, E5M2, xo_gw, xo_gs, E2M1) for t in range(PACK)]
         xt_gw = gather("xt_gw", xt_w, l1, J, U32)
-        w_sd = deal(nc.vector.tensor_copy, "w_sd", w_s, U8)
-        a_rows = [product(t, 4 + t, "a%d" % t, w_wd, w_sd, E2M1, xt_gw, xt_gs, E4M3) for t in range(PACK)]
-
+        xt_gs = gather("xt_gs", xt_s, l1, J, U8)
         x7_gw = gather("x7_gw", xt_w, l7, O, U32)
         x7_gs = gather("x7_gs", xt_s, l7, O, U8)
+        a_rows = [product(t, 4 + t, "a%d" % t, w_wd, w_sd, E2M1, xt_gw, xt_gs, E4M3) for t in range(PACK)]
+
         y_ps = [psum.tile([P, O], F32, name="y%d_ps" % h, tag="bank%d" % h) for h in range(2)]
         for h in range(2):
             cols = slice(h * P, (h + 1) * P)
             nc.tensor.matmul_mx(out=y_ps[h][:], lhsT=ws_w[:, cols].bitcast(E5M2), lhsT_scale=ws_s[:, cols],
                                 rhs=x7_gw[:].bitcast(E4M3), rhs_scale=x7_gs[:], start=True, stop=False)
 
-        val = [tile("val%d" % t, [P, 2, O], F32) for t in range(PACK)]
-        gate = [tile("gate%d" % t, [P, 2, O], F32) for t in range(PACK)]
+        def look(name, rows, offsets, func, t, **factors):
+            dst = tile("%s%d" % (name, t), [P, O], F32)
+            columns = {key: vec[:, t : t + 1] for key, vec in factors.items()}
+            nc.scalar.activation(dst[:], rows[t][:].indirect(offsets[:]), func, **columns)
+            return dst
+
+        gate1 = [look("gate1_", b_rows, l4, ACT.Sigmoid, t, bias=bg_t, scale=sg_t) for t in range(PACK)]
+        val2 = [look("val2_", b_rows, l5, ACT.Copy, t, scale=sb_t) for t in range(PACK)]
+        u1, u2, diff = (tile(name, [P, PACK, O], F32) for name in ("u1", "u2", "diff"))
         for t in range(PACK):
-            nc.scalar.activation(gate[t][:, 0, :], b_rows[t][:].indirect(l4[:]), ACT.Sigmoid,
-                                 bias=bg_t[:, t : t + 1], scale=sg_t[:, t : t + 1])
-        for t in range(PACK):
-            nc.scalar.activation(val[t][:, 1, :], b_rows[t][:].indirect(l5[:]), ACT.Copy, scale=sb_t[:, t : t + 1])
-        diff = tile("diff", [P, PACK, O], F32)
-        for t in range(PACK):
-            nc.scalar.activation(gate[t][:, 1, :], a_rows[t][:].indirect(l6[:]), ACT.Sigmoid,
-                                 bias=bh_t[:, t : t + 1], scale=sh_t[:, t : t + 1])
-            nc.scalar.activation(val[t][:, 0, :], a_rows[t][:].indirect(l3[:]), ACT.Copy, scale=sa_t[:, t : t + 1])
-            u = tile("u%d" % t, [P, 2, O], F32)
-            if t < PACK - 1:
-                nc.vector.tensor_tensor(u[:], val[t][:], gate[t][:], ALU.mult)
-            else:
-                nc.vector.tensor_tensor(u[:, 1, :], val[t][:, 1, :], gate[t][:, 1, :], ALU.mult)
-                nc.vector.tensor_tensor(u[:, 0, :], val[t][:, 0, :], gate[t][:, 0, :], ALU.mult)
-            nc.vector.tensor_tensor(diff[:, t, :], u[:, 0, :], u[:, 1, :], ALU.subtract)
+            val1 = look("val1_", a_rows, l3, ACT.Copy, t, scale=sa_t)
+            nc.vector.tensor_tensor(u1[:, t, :], val1[:], gate1[t][:], ALU.mult)
+        for t in range(PACK + 2):
+            if t < PACK:
+                gate2 = look("gate2_", a_rows, l6, ACT.Sigmoid, t, bias=bh_t, scale=sh_t)
+                nc.vector.tensor_tensor(u2[:, t, :], val2[t][:], gate2[:], ALU.mult)
+            if t >= 2:
+                nc.vector.tensor_tensor(diff[:, t - 2, :], u1[:, t - 2, :], u2[:, t - 2, :], ALU.subtract)
 
         hid = tile("hid", [P, O, PACK], BF16)
         for e in range(0, PACK, 2):

@@ -30,8 +30,8 @@ def tile_list_gatedcross_twotab_further_plain_kernel(
         keep = ctx.enter_context(tc.tile_pool(name="keep", bufs=1))
         psum = ctx.enter_context(tc.psum_pool(name="psum", bufs=1))
 
-        def tile(name, shape, dtype):
-            return keep.tile(shape, dtype, name=name, align_bytes=64)
+        def tile(name, shape, dtype, tag=None):
+            return keep.tile(shape, dtype, name=name, tag=tag or name, align_bytes=64)
 
         def load_list(name, src):
             dst = keep.tile(list(src.shape), U16, name=name)
@@ -58,20 +58,21 @@ def tile_list_gatedcross_twotab_further_plain_kernel(
                 nc.vector.tensor_copy(plane[32 * q : 32 * q + 4, :].bitcast(I32), stage[:, q, :].bitcast(I32))
 
         def load_plane(plane, src):
-            for q in range(4):
-                nc.sync.dma_start(plane[32 * q : 32 * q + 4, :].bitcast(I32), src[0, 4 * q : 4 * q + 4, :].bitcast(I32))
+            for r in range(4):
+                nc.sync.dma_start(plane[r:P:32, :].bitcast(I32), src[0, r:16:4, :].bitcast(I32))
 
-        def load_rows(name, src):
+        def load_rows(queue, name, src):
             dst = keep.tile([P, PACK], F32, name=name)
-            nc.sync.dma_start(dst[:], src.rearrange("(p t) one -> p (t one)", t=PACK))
+            queue.dma_start(dst[:], src.rearrange("(p t) one -> p (t one)", t=PACK))
             return dst
 
-        def deal(copy, dst, src, slots):
-            by_slot = dst[:].rearrange("p (t m) -> p m t", t=PACK)
-            copy(by_slot[:, :, slots], src[:].rearrange("p (m t) -> p m t", t=PACK)[:, :, slots])
+        def deal(copy, name, src, dtype, first, count, tag=None):
+            dst = tile(name, [P, count, P], dtype, tag)
+            copy(dst[:].rearrange("p t m -> p m t"), src[:].rearrange("p (m t) -> p m t", t=PACK)[:, :, first : first + count])
+            return [dst[:, t, :] for t in range(count)]
 
-        def gather(name, window, offsets, count, dtype):
-            dst = tile(name, [P, count], dtype)
+        def gather(name, window, offsets, count, dtype, tag=None):
+            dst = tile(name, [P, count], dtype, tag)
             nc.vector.tensor_copy(dst[:], window[:].indirect(offsets[:]))
             return dst
 
@@ -94,19 +95,18 @@ def tile_list_gatedcross_twotab_further_plain_kernel(
         load_plane(xo_s, xo_scales)
         w2_w = load_words("w2_w", flat(w2_words), R, U32)
         w_w = load_words("w_w", w_words[0], R, U16)
-        w_stage = load_stage("w_stage", w_scales, R)
         l4 = load_list("l4", offs4)
-        sg_t, bg_t = load_rows("sg_t", sg), load_rows("bg_t", bg)
+        load_plane(w_s, w_scales)
+        sg_t, bg_t, sb_t = (load_rows(nc.gpsimd, n, v) for n, v in (("sg_t", sg), ("bg_t", bg), ("sb_t", sb)))
         xt_w = load_words("xt_w", flat(xt_words), T, U32)
         l1 = load_list("l1", offs)
         load_plane(xt_s, xt_scales)
         l7 = load_list("l7", offs7)
         l5 = load_list("l5", offs5)
-        sb_t = load_rows("sb_t", sb)
         l3 = load_list("l3", offs3)
-        sa_t = load_rows("sa_t", sa)
+        sa_t = load_rows(nc.sync, "sa_t", sa)
         l6 = load_list("l6", offs6)
-        sh_t, bh_t = load_rows("sh_t", sh), load_rows("bh_t", bh)
+        sh_t, bh_t = load_rows(nc.sync, "sh_t", sh), load_rows(nc.sync, "bh_t", bh)
         ws_w = load_words("ws_w", flat(ws_words), N, U32)
         wb_w = load_words("wb_w", flat(wb_words), N, U32)
         load_plane(ws_s, ws_scales)
@@ -114,24 +114,21 @@ def tile_list_gatedcross_twotab_further_plain_kernel(
 
         spread(w2_s, w2_stage)
         xo_gw = gather("xo_gw", xo_w, l2, J, U16)
-        w2_sd, w2_wd = tile("w2_sd", [P, R], U8), tile("w2_wd", [P, R], U32)
-        w_sd, w_wd = tile("w_sd", [P, R], U8), tile("w_wd", [P, R], U16)
-        deal(nc.vector.tensor_copy, w2_sd, w2_s, slice(0, 2))
+        w2_sd = deal(nc.vector.tensor_copy, "w2_sd0", w2_s, U8, 0, 2)
         xo_gs = gather("xo_gs", xo_s, l2, J, U8)
-        deal(nc.vector.tensor_copy, w2_sd, w2_s, slice(2, 4))
-        deal(nc.scalar.copy, w2_wd, w2_w, slice(0, 2))
-        deal(nc.scalar.copy, w2_wd, w2_w, slice(2, 4))
-        deal(nc.scalar.copy, w_wd, w_w, slice(0, 4))
-        spread(w_s, w_stage)
-        nc.gpsimd.tensor_copy(w_sd[:].rearrange("p (t m) -> p t m", t=PACK), w_s[:].rearrange("p (m t) -> p t m", t=PACK))
+        w2_sd = w2_sd + deal(nc.vector.tensor_copy, "w2_sd1", w2_s, U8, 2, 2, "xo_s")
+        w2_wd = deal(nc.scalar.copy, "w2_wd0", w2_w, U32, 0, 2) + deal(nc.scalar.copy, "w2_wd1", w2_w, U32, 2, 2)
+        w_wd = deal(nc.scalar.copy, "w_wd", w_w, U16, 0, PACK)
+        w_sd_tile = tile("w_sd", [P, PACK, P], U8)
+        nc.gpsimd.tensor_copy(w_sd_tile[:], w_s[:].rearrange("p (m t) -> p t m", t=PACK))
+        w_sd = [w_sd_tile[:, t, :] for t in range(PACK)]
 
         def product(t, bank, name, wd, sd, wfmt, gw, gs, gfmt):
             acc = psum.tile([P, J], F32, name=name + "_ps", tag="bank%d" % bank)
-            cols = slice(t * P, (t + 1) * P)
-            nc.tensor.matmul_mx(out=acc[:], lhsT=wd[:, cols].bitcast(wfmt), lhsT_scale=sd[:, cols],
+            nc.tensor.matmul_mx(out=acc[:], lhsT=wd[t].bitcast(wfmt), lhsT_scale=sd[t],
                                 rhs=gw[:].bitcast(gfmt), rhs_scale=gs[:], start=True, stop=True)
-            rows = tile(name, [P, J], F32)
-            (nc.scalar.copy if name == "b0" else nc.vector.tensor_copy)(rows[:], acc[:])
+            rows = tile(name, [P, J], F32, {"a0": "xt_w", "a1": "xt_s"}.get(name))
+            nc.vector.tensor_copy(rows[:], acc[:])
             return rows
 
         b_rows = [product(t, t, "b%d" % t, w2_wd, w2_sd, E5M2, xo_gw, xo_gs, E2M1) for t in range(PACK)]
@@ -141,38 +138,45 @@ def tile_list_gatedcross_twotab_further_plain_kernel(
         x7_gs = gather("x7_gs", xt_s, l7, O, U8)
         a_rows = [product(t, 4 + t, "a%d" % t, w_wd, w_sd, E2M1, xt_gw, xt_gs, E4M3) for t in range(PACK)]
 
+        def look(dst, rows, offsets, func, t, **factors):
+            columns = {key: vec[:, t : t + 1] for key, vec in factors.items()}
+            nc.scalar.activation(dst, rows[t][:].indirect(offsets), func, **columns)
+
+        gate1, val2, val1, gate2 = (
+            [tile("%s%d" % (name, t), [P, O], F32) for t in range(PACK)] for name in ("gate1_", "val2_", "val1_", "gate2_")
+        )
+        u1, u2, diff = (tile(name, [P, PACK, O], F32) for name in ("u1", "u2", "diff"))
+        for t in range(PACK):
+            look(gate1[t][:], b_rows, l4[:], ACT.Sigmoid, t, bias=bg_t, scale=sg_t)
+        for t in range(PACK):
+            look(val2[t][:], b_rows, l5[:], ACT.Copy, t, scale=sb_t)
+        for t in range(PACK):
+            look(val1[t][:], a_rows, l3[:], ACT.Copy, t, scale=sa_t)
+            nc.vector.tensor_tensor(u1[:, t, :], val1[t][:], gate1[t][:], ALU.mult)
+
+        half = O // 2
+        pieces = [(t, 0, O) for t in range(PACK - 1)] + [(PACK - 1, 0, half), (PACK - 1, half, O)]
+        for i in range(len(pieces) + 1):
+            if i < len(pieces):
+                t, lo, hi = pieces[i]
+                look(gate2[t][:, lo:hi], a_rows, l6[:, lo // 16 : hi // 16], ACT.Sigmoid, t, bias=bh_t, scale=sh_t)
+                nc.vector.tensor_tensor(u2[:, t, lo:hi], val2[t][:, lo:hi], gate2[t][:, lo:hi], ALU.mult)
+            if i >= 1:
+                t, lo, hi = pieces[i - 1]
+                nc.vector.tensor_tensor(diff[:, t, lo:hi], u1[:, t, lo:hi], u2[:, t, lo:hi], ALU.subtract)
+
+        hid = tile("hid", [P, O, PACK], BF16)
+        for e, lo, hi in ((0, 0, O), (2, 0, half), (2, half, O)):
+            nc.scalar.activation(hid[:, lo:hi, e : e + 2], diff[:, e : e + 2, lo:hi].rearrange("p t o -> p o t"), ACT.Abs)
+        hid_w = tile("hid_w", [P, O], U32)
+        hid_s = tile("hid_s", [P, O], U8)
+        nc.vector.quantize_mx(out=hid_w[:].bitcast(E4M3), scales=hid_s[:], in_=hid[:].rearrange("p o t -> p (o t)"))
+
         y_ps = [psum.tile([P, O], F32, name="y%d_ps" % h, tag="bank%d" % h) for h in range(2)]
         for h in range(2):
             cols = slice(h * P, (h + 1) * P)
             nc.tensor.matmul_mx(out=y_ps[h][:], lhsT=ws_w[:, cols].bitcast(E5M2), lhsT_scale=ws_s[:, cols],
                                 rhs=x7_gw[:].bitcast(E4M3), rhs_scale=x7_gs[:], start=True, stop=False)
-
-        def look(name, rows, offsets, func, t, **factors):
-            dst = tile("%s%d" % (name, t), [P, O], F32)
-            columns = {key: vec[:, t : t + 1] for key, vec in factors.items()}
-            nc.scalar.activation(dst[:], rows[t][:].indirect(offsets[:]), func, **columns)
-            return dst
-
-        gate1 = [look("gate1_", b_rows, l4, ACT.Sigmoid, t, bias=bg_t, scale=sg_t) for t in range(PACK)]
-        val2 = [look("val2_", b_rows, l5, ACT.Copy, t, scale=sb_t) for t in range(PACK)]
-        u1, u2, diff = (tile(name, [P, PACK, O], F32) for name in ("u1", "u2", "diff"))
-        for t in range(PACK):
-            val1 = look("val1_", a_rows, l3, ACT.Copy, t, scale=sa_t)
-            nc.vector.tensor_tensor(u1[:, t, :], val1[:], gate1[t][:], ALU.mult)
-        for t in range(PACK + 2):
-            if t < PACK:
-                gate2 = look("gate2_", a_rows, l6, ACT.Sigmoid, t, bias=bh_t, scale=sh_t)
-                nc.vector.tensor_tensor(u2[:, t, :], val2[t][:], gate2[:], ALU.mult)
-            if t >= 2:
-                nc.vector.tensor_tensor(diff[:, t - 2, :], u1[:, t - 2, :], u2[:, t - 2, :], ALU.subtract)
-
-        hid = tile("hid", [P, O, PACK], BF16)
-        for e in range(0, PACK, 2):
-            nc.scalar.activation(hid[:, :, e : e + 2], diff[:, e : e + 2, :].rearrange("p t o -> p o t"), ACT.Abs)
-        hid_w = tile("hid_w", [P, O], U32)
-        hid_s = tile("hid_s", [P, O], U8)
-        nc.vector.quantize_mx(out=hid_w[:].bitcast(E4M3), scales=hid_s[:], in_=hid[:].rearrange("p o t -> p (o t)"))
-
         copies = (nc.vector.tensor_copy, nc.scalar.copy)
         queues = (nc.sync, nc.scalar)
         for h in range(2):

from contextlib import ExitStack

import concourse.mybir as mybir

F32 = mybir.dt.float32
BF16 = mybir.dt.bfloat16
I32 = mybir.dt.int32
U32 = mybir.dt.uint32
U16 = mybir.dt.uint16
U8 = mybir.dt.uint8
E4M3 = mybir.dt.float8_e4m3fn_x4
E5M2 = mybir.dt.float8_e5m2_x4
E2M1 = mybir.dt.float4_e2m1fn_x4
ACT = mybir.ActivationFunctionType
ALU = mybir.AluOpType

P = 128
PACK = 4
T, J, R, Z, O, N = 1024, 256, 512, 1024, 128, 256
FLOPS = 335544320


def tile_list_gatedcross_twotab_further_plain_kernel(
    tc, xt_words, xt_scales, xo_words, xo_scales, w_words, w_scales, w2_words, w2_scales,
    sa, sb, sg, bg, sh, bh, wb_words, wb_scales, ws_words, ws_scales,
    offs, offs2, offs3, offs4, offs5, offs6, offs7, out,
):
    nc = tc.nc
    with ExitStack() as ctx:
        keep = ctx.enter_context(tc.tile_pool(name="keep", bufs=1))
        psum = ctx.enter_context(tc.psum_pool(name="psum", bufs=1))

        def tile(name, shape, dtype, tag=None):
            return keep.tile(shape, dtype, name=name, tag=tag or name, align_bytes=64)

        def load_list(name, src):
            dst = keep.tile(list(src.shape), U16, name=name)
            nc.sync.dma_start(dst[:], src)
            return dst

        def load_words(name, src, columns, dtype):
            dst = tile(name, [P, columns], dtype)
            nc.sync.dma_start(dst[:].bitcast(I32), src.bitcast(I32))
            return dst

        def zeroed_plane(name, columns):
            plane = tile(name, [P, columns], U8)
            nc.vector.memset(plane[:].bitcast(I32), 0)
            return plane

        def load_stage(name, src, columns):
            stage = tile(name, [4, 4, columns], U8)
            nc.sync.dma_start(stage[:].bitcast(I32), src[0].rearrange("(q r) n -> r q n", r=4).bitcast(I32))
            return stage

        def spread(plane, stage):
            for q in range(4):
                nc.vector.tensor_copy(plane[32 * q : 32 * q + 4, :].bitcast(I32), stage[:, q, :].bitcast(I32))

        def load_plane(plane, src):
            for r in range(4):
                nc.sync.dma_start(plane[r:P:32, :].bitcast(I32), src[0, r:16:4, :].bitcast(I32))

        def load_rows(queue, name, src):
            dst = keep.tile([P, PACK], F32, name=name)
            queue.dma_start(dst[:], src.rearrange("(p t) one -> p (t one)", t=PACK))
            return dst

        def deal(copy, name, src, dtype, first, count, tag=None):
            dst = tile(name, [P, count, P], dtype, tag)
            copy(dst[:].rearrange("p t m -> p m t"), src[:].rearrange("p (m t) -> p m t", t=PACK)[:, :, first : first + count])
            return [dst[:, t, :] for t in range(count)]

        def gather(name, window, offsets, count, dtype, tag=None):
            dst = tile(name, [P, count], dtype, tag)
            nc.vector.tensor_copy(dst[:], window[:].indirect(offsets[:]))
            return dst

        def flat(words):
            return words[0].rearrange("p n t -> p (n t)")

        xo_s = zeroed_plane("xo_s", Z)
        w2_s = zeroed_plane("w2_s", R)
        xt_s = zeroed_plane("xt_s", T)
        w_s = zeroed_plane("w_s", R)
        ws_s = zeroed_plane("ws_s", N)
        wb_s = zeroed_plane("wb_s", N)

        warm = tile("warm", [P, 2], F32)
        nc.vector.memset(warm[:, 0:1], 0.0)
        nc.scalar.activation(warm[:, 1:2], warm[:, 0:1], ACT.Sigmoid)
        w2_stage = load_stage("w2_stage", w2_scales, R)
        xo_w = load_words("xo_w", xo_words[0], Z, U16)
        l2 = load_list("l2", offs2)
        load_plane(xo_s, xo_scales)
        w2_w = load_words("w2_w", flat(w2_words), R, U32)
        w_w = load_words("w_w", w_words[0], R, U16)
        l4 = load_list("l4", offs4)
        load_plane(w_s, w_scales)
        sg_t, bg_t, sb_t = (load_rows(nc.gpsimd, n, v) for n, v in (("sg_t", sg), ("bg_t", bg), ("sb_t", sb)))
        xt_w = load_words("xt_w", flat(xt_words), T, U32)
        l1 = load_list("l1", offs)
        load_plane(xt_s, xt_scales)
        l7 = load_list("l7", offs7)
        l5 = load_list("l5", offs5)
        l3 = load_list("l3", offs3)
        sa_t = load_rows(nc.sync, "sa_t", sa)
        l6 = load_list("l6", offs6)
        sh_t, bh_t = load_rows(nc.sync, "sh_t", sh), load_rows(nc.sync, "bh_t", bh)
        ws_w = load_words("ws_w", flat(ws_words), N, U32)
        wb_w = load_words("wb_w", flat(wb_words), N, U32)
        load_plane(ws_s, ws_scales)
        load_plane(wb_s, wb_scales)

        spread(w2_s, w2_stage)
        xo_gw = gather("xo_gw", xo_w, l2, J, U16)
        w2_sd = deal(nc.vector.tensor_copy, "w2_sd0", w2_s, U8, 0, 2)
        xo_gs = gather("xo_gs", xo_s, l2, J, U8)
        w2_sd = w2_sd + deal(nc.vector.tensor_copy, "w2_sd1", w2_s, U8, 2, 2, "xo_s")
        w2_wd = deal(nc.scalar.copy, "w2_wd0", w2_w, U32, 0, 2) + deal(nc.scalar.copy, "w2_wd1", w2_w, U32, 2, 2)
        w_wd = deal(nc.scalar.copy, "w_wd", w_w, U16, 0, PACK)
        w_sd_tile = tile("w_sd", [P, PACK, P], U8)
        nc.gpsimd.tensor_copy(w_sd_tile[:], w_s[:].rearrange("p (m t) -> p t m", t=PACK))
        w_sd = [w_sd_tile[:, t, :] for t in range(PACK)]

        def product(t, bank, name, wd, sd, wfmt, gw, gs, gfmt):
            acc = psum.tile([P, J], F32, name=name + "_ps", tag="bank%d" % bank)
            nc.tensor.matmul_mx(out=acc[:], lhsT=wd[t].bitcast(wfmt), lhsT_scale=sd[t],
                                rhs=gw[:].bitcast(gfmt), rhs_scale=gs[:], start=True, stop=True)
            rows = tile(name, [P, J], F32, {"a0": "xt_w", "a1": "xt_s"}.get(name))
            nc.vector.tensor_copy(rows[:], acc[:])
            return rows

        b_rows = [product(t, t, "b%d" % t, w2_wd, w2_sd, E5M2, xo_gw, xo_gs, E2M1) for t in range(PACK)]
        xt_gw = gather("xt_gw", xt_w, l1, J, U32)
        xt_gs = gather("xt_gs", xt_s, l1, J, U8)
        x7_gw = gather("x7_gw", xt_w, l7, O, U32)
        x7_gs = gather("x7_gs", xt_s, l7, O, U8)
        a_rows = [product(t, 4 + t, "a%d" % t, w_wd, w_sd, E2M1, xt_gw, xt_gs, E4M3) for t in range(PACK)]

        def look(dst, rows, offsets, func, t, **factors):
            columns = {key: vec[:, t : t + 1] for key, vec in factors.items()}
            nc.scalar.activation(dst, rows[t][:].indirect(offsets), func, **columns)

        gate1, val2, val1, gate2 = (
            [tile("%s%d" % (name, t), [P, O], F32) for t in range(PACK)] for name in ("gate1_", "val2_", "val1_", "gate2_")
        )
        u1, u2, diff = (tile(name, [P, PACK, O], F32) for name in ("u1", "u2", "diff"))
        for t in range(PACK):
            look(gate1[t][:], b_rows, l4[:], ACT.Sigmoid, t, bias=bg_t, scale=sg_t)
        for t in range(PACK):
            look(val2[t][:], b_rows, l5[:], ACT.Copy, t, scale=sb_t)
        for t in range(PACK):
            look(val1[t][:], a_rows, l3[:], ACT.Copy, t, scale=sa_t)
            nc.vector.tensor_tensor(u1[:, t, :], val1[t][:], gate1[t][:], ALU.mult)

        half = O // 2
        pieces = [(t, 0, O) for t in range(PACK - 1)] + [(PACK - 1, 0, half), (PACK - 1, half, O)]
        for i in range(len(pieces) + 1):
            if i < len(pieces):
                t, lo, hi = pieces[i]
                look(gate2[t][:, lo:hi], a_rows, l6[:, lo // 16 : hi // 16], ACT.Sigmoid, t, bias=bh_t, scale=sh_t)
                nc.vector.tensor_tensor(u2[:, t, lo:hi], val2[t][:, lo:hi], gate2[t][:, lo:hi], ALU.mult)
            if i >= 1:
                t, lo, hi = pieces[i - 1]
                nc.vector.tensor_tensor(diff[:, t, lo:hi], u1[:, t, lo:hi], u2[:, t, lo:hi], ALU.subtract)

        hid = tile("hid", [P, O, PACK], BF16)
        for e, lo, hi in ((0, 0, O), (2, 0, half), (2, half, O)):
            nc.scalar.activation(hid[:, lo:hi, e : e + 2], diff[:, e : e + 2, lo:hi].rearrange("p t o -> p o t"), ACT.Abs)
        hid_w = tile("hid_w", [P, O], U32)
        hid_s = tile("hid_s", [P, O], U8)
        nc.vector.quantize_mx(out=hid_w[:].bitcast(E4M3), scales=hid_s[:], in_=hid[:].rearrange("p o t -> p (o t)"))

        y_ps = [psum.tile([P, O], F32, name="y%d_ps" % h, tag="bank%d" % h) for h in range(2)]
        for h in range(2):
            cols = slice(h * P, (h + 1) * P)
            nc.tensor.matmul_mx(out=y_ps[h][:], lhsT=ws_w[:, cols].bitcast(E5M2), lhsT_scale=ws_s[:, cols],
                                rhs=x7_gw[:].bitcast(E4M3), rhs_scale=x7_gs[:], start=True, stop=False)
        copies = (nc.vector.tensor_copy, nc.scalar.copy)
        queues = (nc.sync, nc.scalar)
        for h in range(2):
            cols = slice(h * P, (h + 1) * P)
            nc.tensor.matmul_mx(out=y_ps[h][:], lhsT=wb_w[:, cols].bitcast(E5M2), lhsT_scale=wb_s[:, cols],
                                rhs=hid_w[:].bitcast(E4M3), rhs_scale=hid_s[:], start=False, stop=True)
            y = tile("y%d" % h, [P, O], F32)
            copies[h](y[:], y_ps[h][:])
            queues[h].dma_start(out[cols, :], y[:])
